import numpy as np
CORES = [21,85,149,213,277,341,405,469]
N = 8
T = 1024
def entries(a): return a.T.reshape(-1)
def pack(v, P): return np.ascontiguousarray(np.asarray(v, np.int32).reshape(-1, P).T)
def lists(rng, how):
    Q = rng.permutation(N * T)
    if how == "stay": Q = np.arange(N * T)
    if how == "own": Q = np.concatenate([T * r + rng.permutation(T) for r in range(N)])
    if how == "shift": Q = (np.arange(N * T) + T * int(rng.integers(1, N)) + 1) % (N * T)
    if how == "deal": Q = (np.arange(N * T) % N) * T + np.arange(N * T) // N
    if how == "block": s = int(rng.integers(1, N)); Q = np.concatenate([T * ((r + s) % N) + rng.permutation(T) for r in range(N)])
    return {"goes": np.broadcast_to(pack(Q, 16), (N, 16, N * T // 16)).copy()}
def setup_inputs(rng):
    return dict({"x": rng.standard_normal((N, 128, T), dtype=np.float32)}, **lists(rng, "uniform"))
def setup_inputs_block(rng):
    d = setup_inputs(rng); d.update(lists(rng, "block"))
    for k in ("x",): d[k] = (d[k].astype(np.float32) * 1048576.0).astype(d[k].dtype)
    return d
def setup_inputs_deal(rng):
    d = setup_inputs(rng); d.update(lists(rng, "deal"))
    for k in ("x",): d[k] = (d[k].astype(np.float32) * (1 / 1024.0)).astype(d[k].dtype)
    return d
def setup_inputs_own(rng):
    d = setup_inputs(rng); d.update(lists(rng, "own"))
    return d
def setup_inputs_shift(rng):
    d = setup_inputs(rng); d.update(lists(rng, "shift"))
    return d
def setup_inputs_stay(rng):
    d = setup_inputs(rng); d.update(lists(rng, "stay"))
    return d
def check_inputs(x):
    bad = []
    if x["goes"].min() < 0 or x["goes"].max() >= N * T: bad.append("goes out of range")
    if not np.array_equal(np.sort(entries(x["goes"][0])), np.arange(N * T)): bad.append("goes isn't a permutation")
    if not all(np.array_equal(a, x["goes"][0]) for a in x["goes"]): bad.append("goes isn't alike on all ranks")
    return bad
def reference(x, goes):
    A = np.concatenate(list(x), axis=1); Y = np.zeros_like(A)
    Y[:, entries(goes[0])] = A
    return {"y": np.stack([Y[:, T * r:T * r + T] for r in range(N)])}

@@ -1,0 +1,252 @@
+from concourse.bass import DstId, RemoteDMATransfer
+from concourse.mybir import AluOpType
+
+N = 8
+TC = 1024
+NSIM = 512
+K = 4
+WC = TC // K
+
+SCRATCH = {
+    "Wd": ("sbuf", [128, 5 * TC], "float32"),
+    "Pb": ("sbuf", [128, TC], "float32"),
+    "Y": ("sbuf", [128, TC], "float32"),
+    "Hx": ("sbuf", [128, WC], "float32"),
+    "Hp": ("sbuf", [128, WC], "float32"),
+    "G32": ("sbuf", [128, 32], "int32"),
+    "off16": ("sbuf", [128, 32], "uint16"),
+    "V": ("sbuf", [128, 512], "float32"),
+    "Wi": ("sbuf", [128, N * TC], "float32"),
+    "Wi8": ("sbuf", [128, 8], "int32"),
+    "Wsel": ("sbuf", [128, 8], "float32"),
+    "SelI": ("sbuf", [128, 128], "int32"),
+    "Sel": ("sbuf", [128, 128], "float32"),
+    "MaskI": ("sbuf", [128, 128], "int32"),
+    "Mask": ("sbuf", [128, 128], "float32"),
+    "Jt": ("sbuf", [128, 128], "float32"),
+    "R1": ("sbuf", [128, 128], "float32"),
+    "R2": ("sbuf", [128, 128], "float32"),
+    "offAB": ("sbuf", [128, 128], "uint16"),
+    "PS1": ("psum", [128, 512], "float32"),
+    "PS2": ("psum", [128, 512], "float32"),
+}
+SEMAPHORES = (["ldh", "ldo", "lg", "iV", "iW", "iS", "iM", "iJ", "mA", "mB", "w1", "w2", "o1", "sc", "pe1", "s1", "s2",
+               "m1", "m2", "j2", "r1", "r2", "pe2", "ob", "ag", "hx", "hp", "loc"]
+              + ["%s%d" % (n, k) for n in ("gb", "cb", "ga", "st") for k in range(K)])
+
+PLAN = {}
+
+
+def engines(mask, count, top=0):
+    bits = [b for b in range(16) if (mask >> b) & 1]
+    bits = bits[len(bits) - top - count:len(bits) - top]
+    return sum(1 << b for b in bits)
+
+
+def pow2_le(n):
+    p = 1
+    while p * 2 <= n:
+        p *= 2
+    return p
+
+
+def nbits(mask):
+    return sum((mask >> b) & 1 for b in range(16))
+
+
+def plan(T, topo):
+    if "p" in PLAN:
+        return PLAN["p"]
+    cores = [int(c) for c in T.cores]
+    ranks, helper = {}, {}
+    for r, c in enumerate(cores):
+        rk = [q for q in range(N) if topo.rack(topo.host(cores[q])) == topo.rack(topo.host(c))]
+        pa = [q for q in range(N) if q not in rk and topo.chip(cores[q]) == topo.chip(c) and topo.may_write(c, cores[q])]
+        assert len(pa) == 1 and rk == list(range(rk[0], rk[0] + len(rk))) and len(rk) == 4
+        assert all(topo.same_plane(c, cores[q]) for q in rk if q != r)
+        hostc = [m for m in range(NSIM) if topo.host(m) == topo.host(c)]
+        chipc = [m for m in hostc if topo.chip(m) == topo.chip(c)]
+
+        def kind(k):
+            return (topo.die(k), any(topo.may_write(k, m) for m in hostc if topo.mates(k, m)))
+        kinds = []
+        for m in chipc:
+            if kind(m) not in kinds:
+                kinds.append(kind(m))
+        kinds.sort(key=lambda kd: (kd == kind(c), kd[0] == topo.die(c)))
+        order = []
+        left = [m for m in chipc if m != c]
+        while left:
+            for kd in kinds:
+                mine = [m for m in left if kind(m) == kd]
+                if mine and not (len(order) < len(kinds) - 1 and kd == kind(c)):
+                    order.append(mine[0])
+                    left.remove(mine[0])
+        team = order[:K - 1] + [c]
+        ranks[c] = dict(r=r, rk=rk, partner=pa[0], team=team)
+        for k, h in enumerate(team[:-1]):
+            helper[h] = (c, k)
+    PLAN["p"] = dict(cores=cores, ranks=ranks, helper=helper)
+    return PLAN["p"]
+
+
+def send_x_slice(g, core, T, topo, P, info, k, src):
+    col = TC * info["rk"].index(info["r"]) + WC * k
+    peers = [P["cores"][q] for q in info["rk"] if q != info["r"]]
+    m = topo.mask(core, peers[0])
+    for d in peers:
+        m &= topo.mask(core, d)
+    m = engines(m, pow2_le(nbits(m)))
+    ids = []
+    for d in peers:
+        rid, pid = topo.addr(d, core)
+        ids.append(DstId(rid=rid, pnc=pid))
+    g.remote_dma_fused([RemoteDMATransfer(dst_ids=ids, dma_engine_mask=m, remote_sem=T.sem.ag, srcs=[src],
+                                          dsts=[T.Wd[:, col:col + WC] for d in peers])], local_sem=T.sem.loc)
+    return nbits(m)
+
+
+def send_block_slice(g, core, T, topo, P, info, k, src):
+    d = P["cores"][info["partner"]]
+    m = topo.mask(core, d)
+    m = engines(m, pow2_le(nbits(m)))
+    rid, pid = topo.addr(d, core)
+    g.remote_dma(out_ap=T.Wd[:, 4 * TC + WC * k:4 * TC + WC * (k + 1)], in_ap=src, remote_sem=T.sem["cb%d" % k],
+                 local_sem=T.sem.loc, pid=pid, routing_id=rid, dma_engine_mask=m)
+    return nbits(m)
+
+
+def hand_masks(core, team, topo):
+    if K == 1:
+        return []
+    full = topo.mask(core, team[0])
+    for h in team[:-1]:
+        full &= topo.mask(core, h)
+    per = pow2_le(nbits(full) // (K - 1))
+    return [engines(full, per, top=per * k) for k in range(K - 1)]
+
+
+def rank_program(g, core, T, topo):
+    P = plan(T, topo)
+    S = T.sem
+    if core in P["helper"]:
+        rc, k = P["helper"][core]
+        info = P["ranks"][rc]
+        hm = hand_masks(rc, info["team"], topo)
+        g.wait_ge(S.hx, nbits(hm[k]))
+        n = send_x_slice(g, core, T, topo, P, info, k, T.Hx[:, :])
+        g.wait_ge(S.hp, nbits(engines(topo.mask(rc, core), pow2_le(nbits(topo.mask(rc, core))))))
+        n += send_block_slice(g, core, T, topo, P, info, k, T.Hp[:, :])
+        g.wait_ge(S.loc, n)
+        return
+    if core not in P["ranks"]:
+        return
+    info = P["ranks"][core]
+    r, rk, pa, team = info["r"], info["rk"], info["partner"], info["team"]
+    own = TC * rk.index(r)
+    hc = WC * (K - 1)
+    a = rk[0] * (TC // 16)
+    v, pe = g.vector, g.tensor
+    A = AluOpType
+
+    if K > 1:
+        g.sync.dma_start(T.Wd[:, own:own + hc], T.x[:, 0:hc]).then_inc(S.ldh, 16)
+    g.sync.dma_start(T.Wd[:, own + hc:own + TC], T.x[:, hc:TC]).then_inc(S.ldo, 16)
+    for gi in range(8):
+        g.scalar.dma_start(T.G32[16 * gi:16 * gi + 16, :], T.goes[:, a + 32 * gi:a + 32 * gi + 32]).then_inc(S.lg, 16)
+
+    g.iota(T.V[:, :], [[1, 512]], -8192, 32, allow_small_or_imprecise_dtypes=True).then_inc(S.iV, 1)
+    g.iota(T.Wi8[:, :], [[0, 8]], 0, 1).then_inc(S.iW, 1)
+    nloc = 0
+    if K > 1:
+        hm = hand_masks(core, team, topo)
+        trs = []
+        for k, h in enumerate(team[:-1]):
+            rid, pid = topo.addr(h, core)
+            trs.append(RemoteDMATransfer(dst_ids=[DstId(rid=rid, pnc=pid)], dma_engine_mask=hm[k], remote_sem=S.hx,
+                                         src=T.Wd[:, own + WC * k:own + WC * (k + 1)], dst=T.Hx[:, :]))
+            nloc += nbits(hm[k])
+        g.wait_ge(S.ldh, 16)
+        g.remote_dma_fused(trs, local_sem=S.loc)
+    g.wait_ge(S.ldo, 16)
+    nag = send_x_slice(g, core, T, topo, P, info, K - 1, T.Wd[:, own + hc:own + TC])
+    nloc += nag
+    g.iota(T.Jt[:, 0:64], [[128, 8], [0, 8]], -4096, 1, allow_small_or_imprecise_dtypes=True).then_inc(S.iJ, 1)
+    g.iota(T.MaskI[:, :], [[0, 16], [-16, 8]], 128, 1).then_inc(S.iM, 1)
+    g.iota(T.SelI[:, :], [[-1, 128]], 128, 1).then_inc(S.iS, 1)
+
+    v.memset(T.Wi[:, TC * pa:TC * pa + TC], 0.0).then_inc(S.mB, 1)
+    v.memset(T.Wi[:, TC * r:TC * r + TC], 0.0).then_inc(S.mA, 1)
+    v.memset(T.Jt[:, 64:128], -4097.0).then_inc(S.j2, 1)
+    v.wait_ge(S.iW, 1)
+    v.tensor_scalar(T.Wi8[:, :], T.Wi8[:, :], 15, None, A.bitwise_and).then_inc(S.w1, 1)
+    v.wait_ge(S.w1, 1)
+    v.tensor_scalar(T.Wsel[:, :], T.Wi8[:, :], 0, None, A.is_equal).then_inc(S.w2, 1)
+    v.wait_ge(S.lg, 128)
+    v.tensor_copy(T.off16[:, :], T.G32[:, :]).then_inc(S.o1, 1)
+    v.wait_ge(S.o1, 1)
+    v.wait_ge(S.iV, 1)
+    v.wait_ge(S.mA, 1)
+    v.wait_ge(S.mB, 1)
+    v.tensor_copy(T.Wi[:, 0:N * TC].indirect(T.off16[:, 0:32]), T.V[:, :]).then_inc(S.sc, 1)
+
+    pe.wait_ge(S.sc, 1)
+    pe.wait_ge(S.w2, 1)
+    for li, base in enumerate((TC * r, TC * pa)):
+        for b in range(8):
+            pe.matmul(T.PS1[:, 64 * li + 8 * b:64 * li + 8 * b + 8], T.Wi[:, base + 128 * b:base + 128 * b + 128],
+                      T.Wsel[:, :], True, True).then_inc(S.pe1, 1)
+
+    v.wait_ge(S.iM, 1)
+    v.tensor_scalar(T.MaskI[:, :], T.MaskI[:, :], 4, None, A.logical_shift_right).then_inc(S.m1, 1)
+    v.wait_ge(S.iS, 1)
+    v.tensor_scalar(T.SelI[:, :], T.SelI[:, :], 15, None, A.bitwise_and).then_inc(S.s1, 1)
+    v.wait_ge(S.m1, 1)
+    v.tensor_scalar(T.Mask[:, :], T.MaskI[:, :], 8, None, A.is_equal).then_inc(S.m2, 1)
+    v.wait_ge(S.s1, 1)
+    v.tensor_scalar(T.Sel[:, :], T.SelI[:, :], 0, None, A.is_equal).then_inc(S.s2, 1)
+    v.wait_ge(S.pe1, 16)
+    v.wait_ge(S.iJ, 1)
+    v.wait_ge(S.j2, 1)
+    v.tensor_tensor(T.R1[:, :], T.PS1[:, 0:128], T.Jt[:, :], A.min).then_inc(S.r1, 1)
+    v.wait_ge(S.r1, 1)
+    v.wait_ge(S.m2, 1)
+    v.tensor_tensor(T.R2[:, :], T.R1[:, :], T.Mask[:, :], A.mult).then_inc(S.r2, 1)
+    pe.wait_ge(S.r2, 1)
+    pe.wait_ge(S.s2, 1)
+    pe.matmul(T.PS2[:, 0:128], T.Sel[:, :], T.R2[:, :], True, True).then_inc(S.pe2, 1)
+    v.wait_ge(S.pe2, 1)
+    v.tensor_scalar(T.offAB[:, :], T.PS2[:, 0:128], 8192, None, A.add).then_inc(S.ob, 1)
+    v.wait_ge(S.ob, 1)
+
+    if K > 1:
+        v.wait_ge(S.ldh, 16)
+    v.wait_ge(S.ldo, 16)
+    v.wait_ge(S.ag, 3 * K * nag)
+    oc = WC // 16
+    for k in range(K):
+        v.tensor_copy(T.Pb[:, WC * k:WC * (k + 1)],
+                      T.Wd[:, 0:4 * TC].indirect(T.offAB[:, 64 + oc * k:64 + oc * (k + 1)])).then_inc(S["gb%d" % k], 1)
+    for k in range(K):
+        g.wait_ge(S["gb%d" % k], 1)
+        if k < K - 1:
+            h = team[k]
+            m = engines(topo.mask(core, h), pow2_le(nbits(topo.mask(core, h))))
+            rid, pid = topo.addr(h, core)
+            g.remote_dma(out_ap=T.Hp[:, :], in_ap=T.Pb[:, WC * k:WC * (k + 1)], remote_sem=S.hp, local_sem=S.loc,
+                         pid=pid, routing_id=rid, dma_engine_mask=m)
+            nloc += nbits(m)
+        else:
+            ncb = send_block_slice(g, core, T, topo, P, info, k, T.Pb[:, WC * k:WC * (k + 1)])
+            nloc += ncb
+
+    for k in range(K):
+        v.wait_ge(S["cb%d" % k], ncb)
+        v.tensor_copy(T.Y[:, WC * k:WC * (k + 1)],
+                      T.Wd[:, 0:4 * TC + WC * (k + 1)].indirect(T.offAB[:, oc * k:oc * (k + 1)])).then_inc(S["ga%d" % k], 1)
+        q = g.sync if k % 2 == 0 else g.scalar
+        q.wait_ge(S["ga%d" % k], 1)
+        q.dma_start(T.y[:, WC * k:WC * (k + 1)], T.Y[:, WC * k:WC * (k + 1)]).then_inc(S["st%d" % k], 16)
+    g.wait_ge(S.loc, nloc)
+    for k in range(K):
+        g.wait_ge(S["st%d" % k], 16)

@@ -1,17 +1,19 @@
 from concourse.bass import DstId, RemoteDMATransfer
-from concourse.mybir import AluOpType
+from concourse.mybir import AluOpType, ActivationFunctionType
 
 N = 8
 TC = 1024
 NSIM = 512
 K = 4
 WC = TC // K
+NX = 6
+XC = 128
 
 SCRATCH = {
     "Wd": ("sbuf", [128, 5 * TC], "float32"),
     "Pb": ("sbuf", [128, TC], "float32"),
     "Y": ("sbuf", [128, TC], "float32"),
-    "Hx": ("sbuf", [128, WC], "float32"),
+    "Hx": ("sbuf", [128, XC], "float32"),
     "Hp": ("sbuf", [128, WC], "float32"),
     "G32": ("sbuf", [128, 32], "int32"),
     "off16": ("sbuf", [128, 32], "uint16"),
@@ -30,9 +32,9 @@ SCRATCH = {
     "PS1": ("psum", [128, 512], "float32"),
     "PS2": ("psum", [128, 512], "float32"),
 }
-SEMAPHORES = (["ldh", "ldo", "lg", "iV", "iW", "iS", "iM", "iJ", "mA", "mB", "w1", "w2", "o1", "sc", "pe1", "s1", "s2",
+SEMAPHORES = (["lg", "iV", "iW", "iS", "iM", "iJ", "mA", "mB", "w1", "w2", "o1", "sc", "pe1", "s1", "s2",
                "m1", "m2", "j2", "r1", "r2", "pe2", "ob", "ag", "hx", "hp", "loc"]
-              + ["%s%d" % (n, k) for n in ("gb", "cb", "ga", "st") for k in range(K)])
+              + ["%s%d" % (n, k) for n in ("ld", "gb", "cb", "ga", "st") for k in range(K)])
 
 PLAN = {}
 
@@ -66,32 +68,41 @@ def plan(T, topo):
         assert all(topo.same_plane(c, cores[q]) for q in rk if q != r)
         hostc = [m for m in range(NSIM) if topo.host(m) == topo.host(c)]
         chipc = [m for m in hostc if topo.chip(m) == topo.chip(c)]
-
-        def kind(k):
-            return (topo.die(k), any(topo.may_write(k, m) for m in hostc if topo.mates(k, m)))
-        kinds = []
-        for m in chipc:
-            if kind(m) not in kinds:
-                kinds.append(kind(m))
-        kinds.sort(key=lambda kd: (kd == kind(c), kd[0] == topo.die(c)))
-        order = []
-        left = [m for m in chipc if m != c]
+        kd = {}
+        for k in chipc:
+            kd[k] = (topo.die(k), any(topo.may_write(k, m) for m in hostc if topo.mates(k, m)))
+        far = [m for m in chipc if topo.die(m) != topo.die(c)]
+        near = [m for m in chipc if topo.die(m) == topo.die(c) and m != c]
+        near = [m for m in near if kd[m] != kd[c]] + [m for m in near if kd[m] == kd[c]]
+        fk = []
+        for m in far:
+            if kd[m] not in fk:
+                fk.append(kd[m])
+        far2, left = [], list(far)
         while left:
-            for kd in kinds:
-                mine = [m for m in left if kind(m) == kd]
-                if mine and not (len(order) < len(kinds) - 1 and kd == kind(c)):
-                    order.append(mine[0])
+            for q in fk:
+                mine = [m for m in left if kd[m] == q]
+                if mine:
+                    far2.append(mine[0])
                     left.remove(mine[0])
-        team = order[:K - 1] + [c]
-        ranks[c] = dict(r=r, rk=rk, partner=pa[0], team=team)
-        for k, h in enumerate(team[:-1]):
-            helper[h] = (c, k)
+        nf = min(len(far2), (TC // 2) // XC)
+        car = far2[:nf] + near[:NX - nf]
+        assert len(car) == NX
+        cab, seen = [], [kd[c]]
+        for m in car:
+            if kd[m] not in seen:
+                seen.append(kd[m])
+                cab.append(m)
+        assert len(cab) == K - 1
+        ranks[c] = dict(r=r, rk=rk, partner=pa[0], car=car, cab=cab)
+        for i, h in enumerate(car):
+            helper[h] = (c, i, cab.index(h) if h in cab else None)
     PLAN["p"] = dict(cores=cores, ranks=ranks, helper=helper)
     return PLAN["p"]
 
 
-def send_x_slice(g, core, T, topo, P, info, k, src):
-    col = TC * info["rk"].index(info["r"]) + WC * k
+def send_x_slice(g, core, T, topo, P, info, c0, w, src):
+    col = TC * info["rk"].index(info["r"]) + c0
     peers = [P["cores"][q] for q in info["rk"] if q != info["r"]]
     m = topo.mask(core, peers[0])
     for d in peers:
@@ -102,7 +113,7 @@ def send_x_slice(g, core, T, topo, P, info, k, src):
         rid, pid = topo.addr(d, core)
         ids.append(DstId(rid=rid, pnc=pid))
     g.remote_dma_fused([RemoteDMATransfer(dst_ids=ids, dma_engine_mask=m, remote_sem=T.sem.ag, srcs=[src],
-                                          dsts=[T.Wd[:, col:col + WC] for d in peers])], local_sem=T.sem.loc)
+                                          dsts=[T.Wd[:, col:col + w] for d in peers])], local_sem=T.sem.loc)
     return nbits(m)
 
 
@@ -116,60 +127,57 @@ def send_block_slice(g, core, T, topo, P, info, k, src):
     return nbits(m)
 
 
-def hand_masks(core, team, topo):
-    if K == 1:
-        return []
-    full = topo.mask(core, team[0])
-    for h in team[:-1]:
-        full &= topo.mask(core, h)
-    per = pow2_le(nbits(full) // (K - 1))
-    return [engines(full, per, top=per * k) for k in range(K - 1)]
+def pair_masks(core, a, b, topo):
+    full = topo.mask(core, a) & topo.mask(core, b)
+    per = pow2_le(nbits(full) // 2)
+    return [engines(full, per, top=0), engines(full, per, top=per)]
 
 
 def rank_program(g, core, T, topo):
     P = plan(T, topo)
     S = T.sem
     if core in P["helper"]:
-        rc, k = P["helper"][core]
+        rc, i, ck = P["helper"][core]
         info = P["ranks"][rc]
-        hm = hand_masks(rc, info["team"], topo)
-        g.wait_ge(S.hx, nbits(hm[k]))
-        n = send_x_slice(g, core, T, topo, P, info, k, T.Hx[:, :])
-        g.wait_ge(S.hp, nbits(engines(topo.mask(rc, core), pow2_le(nbits(topo.mask(rc, core))))))
-        n += send_block_slice(g, core, T, topo, P, info, k, T.Hp[:, :])
+        car = info["car"]
+        pm = pair_masks(rc, car[i - i % 2], car[i - i % 2 + 1], topo)
+        g.wait_ge(S.hx, nbits(pm[i % 2]))
+        n = send_x_slice(g, core, T, topo, P, info, XC * i, XC, T.Hx[:, :])
+        if ck is not None:
+            g.wait_ge(S.hp, nbits(engines(topo.mask(rc, core), pow2_le(nbits(topo.mask(rc, core))))))
+            n += send_block_slice(g, core, T, topo, P, info, ck, T.Hp[:, :])
         g.wait_ge(S.loc, n)
         return
     if core not in P["ranks"]:
         return
     info = P["ranks"][core]
-    r, rk, pa, team = info["r"], info["rk"], info["partner"], info["team"]
+    r, rk, pa, car, cab = info["r"], info["rk"], info["partner"], info["car"], info["cab"]
     own = TC * rk.index(r)
-    hc = WC * (K - 1)
     a = rk[0] * (TC // 16)
-    v, pe = g.vector, g.tensor
+    v, pe, sc = g.vector, g.tensor, g.scalar
     A = AluOpType
 
-    if K > 1:
-        g.sync.dma_start(T.Wd[:, own:own + hc], T.x[:, 0:hc]).then_inc(S.ldh, 16)
-    g.sync.dma_start(T.Wd[:, own + hc:own + TC], T.x[:, hc:TC]).then_inc(S.ldo, 16)
+    for j in range(K):
+        g.sync.dma_start(T.Wd[:, own + WC * j:own + WC * (j + 1)], T.x[:, WC * j:WC * (j + 1)]).then_inc(S["ld%d" % j], 16)
     for gi in range(8):
-        g.scalar.dma_start(T.G32[16 * gi:16 * gi + 16, :], T.goes[:, a + 32 * gi:a + 32 * gi + 32]).then_inc(S.lg, 16)
+        sc.dma_start(T.G32[16 * gi:16 * gi + 16, :], T.goes[:, a + 32 * gi:a + 32 * gi + 32]).then_inc(S.lg, 16)
 
     g.iota(T.V[:, :], [[1, 512]], -8192, 32, allow_small_or_imprecise_dtypes=True).then_inc(S.iV, 1)
     g.iota(T.Wi8[:, :], [[0, 8]], 0, 1).then_inc(S.iW, 1)
     nloc = 0
-    if K > 1:
-        hm = hand_masks(core, team, topo)
+    for j in range(NX // 2):
+        pm = pair_masks(core, car[2 * j], car[2 * j + 1], topo)
         trs = []
-        for k, h in enumerate(team[:-1]):
-            rid, pid = topo.addr(h, core)
-            trs.append(RemoteDMATransfer(dst_ids=[DstId(rid=rid, pnc=pid)], dma_engine_mask=hm[k], remote_sem=S.hx,
-                                         src=T.Wd[:, own + WC * k:own + WC * (k + 1)], dst=T.Hx[:, :]))
-            nloc += nbits(hm[k])
-        g.wait_ge(S.ldh, 16)
+        for e in range(2):
+            i = 2 * j + e
+            rid, pid = topo.addr(car[i], core)
+            trs.append(RemoteDMATransfer(dst_ids=[DstId(rid=rid, pnc=pid)], dma_engine_mask=pm[e], remote_sem=S.hx,
+                                         src=T.Wd[:, own + XC * i:own + XC * (i + 1)], dst=T.Hx[:, :]))
+            nloc += nbits(pm[e])
+        g.wait_ge(S["ld%d" % j], 16)
         g.remote_dma_fused(trs, local_sem=S.loc)
-    g.wait_ge(S.ldo, 16)
-    nag = send_x_slice(g, core, T, topo, P, info, K - 1, T.Wd[:, own + hc:own + TC])
+    g.wait_ge(S["ld%d" % (K - 1)], 16)
+    nag = send_x_slice(g, core, T, topo, P, info, XC * NX, TC - XC * NX, T.Wd[:, own + XC * NX:own + TC])
     nloc += nag
     g.iota(T.Jt[:, 0:64], [[128, 8], [0, 8]], -4096, 1, allow_small_or_imprecise_dtypes=True).then_inc(S.iJ, 1)
     g.iota(T.MaskI[:, :], [[0, 16], [-16, 8]], 128, 1).then_inc(S.iM, 1)
@@ -217,20 +225,25 @@ def rank_program(g, core, T, topo):
     pe.matmul(T.PS2[:, 0:128], T.Sel[:, :], T.R2[:, :], True, True).then_inc(S.pe2, 1)
     v.wait_ge(S.pe2, 1)
     v.tensor_scalar(T.offAB[:, :], T.PS2[:, 0:128], 8192, None, A.add).then_inc(S.ob, 1)
-    v.wait_ge(S.ob, 1)
 
-    if K > 1:
-        v.wait_ge(S.ldh, 16)
-    v.wait_ge(S.ldo, 16)
-    v.wait_ge(S.ag, 3 * K * nag)
+    nall = 3 * (NX + 1) * nag
+    for q in (v, sc):
+        q.wait_ge(S.ob, 1)
+        for j in range(K):
+            q.wait_ge(S["ld%d" % j], 16)
+        q.wait_ge(S.ag, nall)
     oc = WC // 16
     for k in range(K):
-        v.tensor_copy(T.Pb[:, WC * k:WC * (k + 1)],
-                      T.Wd[:, 0:4 * TC].indirect(T.offAB[:, 64 + oc * k:64 + oc * (k + 1)])).then_inc(S["gb%d" % k], 1)
+        out = T.Pb[:, WC * k:WC * (k + 1)]
+        src = T.Wd[:, 0:4 * TC].indirect(T.offAB[:, 64 + oc * k:64 + oc * (k + 1)])
+        if k % 2 == 0:
+            v.tensor_copy(out, src).then_inc(S["gb%d" % k], 1)
+        else:
+            sc.activation(out, src, ActivationFunctionType.Copy).then_inc(S["gb%d" % k], 1)
     for k in range(K):
         g.wait_ge(S["gb%d" % k], 1)
         if k < K - 1:
-            h = team[k]
+            h = cab[k]
             m = engines(topo.mask(core, h), pow2_le(nbits(topo.mask(core, h))))
             rid, pid = topo.addr(h, core)
             g.remote_dma(out_ap=T.Hp[:, :], in_ap=T.Pb[:, WC * k:WC * (k + 1)], remote_sem=S.hp, local_sem=S.loc,
@@ -240,13 +253,22 @@ def rank_program(g, core, T, topo):
             ncb = send_block_slice(g, core, T, topo, P, info, k, T.Pb[:, WC * k:WC * (k + 1)])
             nloc += ncb
 
+    waited = {0: 0, 1: 0}
     for k in range(K):
-        v.wait_ge(S["cb%d" % k], ncb)
-        v.tensor_copy(T.Y[:, WC * k:WC * (k + 1)],
-                      T.Wd[:, 0:4 * TC + WC * (k + 1)].indirect(T.offAB[:, oc * k:oc * (k + 1)])).then_inc(S["ga%d" % k], 1)
-        q = g.sync if k % 2 == 0 else g.scalar
-        q.wait_ge(S["ga%d" % k], 1)
-        q.dma_start(T.y[:, WC * k:WC * (k + 1)], T.Y[:, WC * k:WC * (k + 1)]).then_inc(S["st%d" % k], 16)
+        e = k % 2
+        q = v if e == 0 else sc
+        for kk in range(waited[e], k + 1):
+            q.wait_ge(S["cb%d" % kk], ncb)
+        waited[e] = k + 1
+        out = T.Y[:, WC * k:WC * (k + 1)]
+        src = T.Wd[:, 0:4 * TC + WC * (k + 1)].indirect(T.offAB[:, oc * k:oc * (k + 1)])
+        if e == 0:
+            v.tensor_copy(out, src).then_inc(S["ga%d" % k], 1)
+        else:
+            sc.activation(out, src, ActivationFunctionType.Copy).then_inc(S["ga%d" % k], 1)
+        d = g.sync if e == 0 else sc
+        d.wait_ge(S["ga%d" % k], 1)
+        d.dma_start(T.y[:, WC * k:WC * (k + 1)], T.Y[:, WC * k:WC * (k + 1)]).then_inc(S["st%d" % k], 16)
     g.wait_ge(S.loc, nloc)
     for k in range(K):
         g.wait_ge(S["st%d" % k], 16)

@@ -6,14 +6,17 @@ TC = 1024
 NSIM = 512
 K = 4
 WC = TC // K
-NX = 6
+NX = 7
+NM = 2
 XC = 128
+LD = [(0, 2 * XC), (2 * XC, 2 * XC), (4 * XC, 2 * XC), (6 * XC, XC), (7 * XC, XC)]
 
 SCRATCH = {
     "Wd": ("sbuf", [128, 5 * TC], "float32"),
     "Pb": ("sbuf", [128, TC], "float32"),
     "Y": ("sbuf", [128, TC], "float32"),
     "Hx": ("sbuf", [128, XC], "float32"),
+    "Hr": ("sbuf", [128, 4 * XC], "float32"),
     "Hp": ("sbuf", [128, WC], "float32"),
     "G32": ("sbuf", [128, 32], "int32"),
     "off16": ("sbuf", [128, 32], "uint16"),
@@ -33,8 +36,9 @@ SCRATCH = {
     "PS2": ("psum", [128, 512], "float32"),
 }
 SEMAPHORES = (["lg", "iV", "iW", "iS", "iM", "iJ", "mA", "mB", "w1", "w2", "o1", "sc", "pe1", "s1", "s2",
-               "m1", "m2", "j2", "r1", "r2", "pe2", "ob", "ag", "hx", "hp", "loc"]
-              + ["%s%d" % (n, k) for n in ("ld", "gb", "cb", "ga", "st") for k in range(K)])
+               "m1", "m2", "j2", "r1", "r2", "pe2", "ob", "ag", "hx", "hp", "loc", "rl0", "rl1", "rl2", "rl3", "tb"]
+              + ["ld%d" % k for k in range(len(LD))]
+              + ["%s%d" % (n, k) for n in ("gb", "cb", "ga", "st") for k in range(K)])
 
 PLAN = {}
 
@@ -85,42 +89,85 @@ def plan(T, topo):
                 if mine:
                     far2.append(mine[0])
                     left.remove(mine[0])
-        nf = min(len(far2), (TC // 2) // XC)
-        car = far2[:nf] + near[:NX - nf]
-        assert len(car) == NX
+        snd = [[m for m in side if kd[m][1]][0] for side in (far2, near)]
+        fr = [m for m in far2 if m not in snd]
+        nr = [m for m in near if m not in snd]
+        car = []
+        while fr or nr:
+            for side in (fr, nr):
+                if side:
+                    car.append(side.pop(0))
+        hl = snd + car
+        assert len(snd) == NM and len(hl) == NX
         cab, seen = [], [kd[c]]
-        for m in car:
+        for m in hl:
             if kd[m] not in seen:
                 seen.append(kd[m])
                 cab.append(m)
         assert len(cab) == K - 1
-        ranks[c] = dict(r=r, rk=rk, partner=pa[0], car=car, cab=cab)
-        for i, h in enumerate(car):
+        rel = {}
+        for m in hostc:
+            if topo.mates(m, c) and topo.may_write(m, c):
+                rel.setdefault(topo.die(m), []).append(m)
+        wr = hl + sorted(m for side in rel.values() for m in side)
+        assert len(wr) == len(PIECES)
+        ranks[c] = dict(r=r, rk=rk, partner=pa[0], hl=hl, cab=cab, rel=rel, rdst={}, wr=wr)
+        for i, h in enumerate(hl):
             helper[h] = (c, i, cab.index(h) if h in cab else None)
-    PLAN["p"] = dict(cores=cores, ranks=ranks, helper=helper)
+    relay = {}
+    for c, info in ranks.items():
+        r, rk = info["r"], info["rk"]
+        for e in range(NM):
+            sd = topo.die(info["hl"][e])
+            info["rdst"][e] = []
+            for d in rk:
+                if d == r:
+                    continue
+                dc = cores[d]
+                si = [q for q in rk if q != d].index(r)
+                lst = ranks[dc]["rel"][sd]
+                m = lst[si % len(lst)]
+                assert topo.may_write(info["hl"][e], m)
+                info["rdst"][e].append(m)
+                relay.setdefault(m, []).append((si, dc, rk.index(r), e))
+    PLAN["p"] = dict(cores=cores, ranks=ranks, helper=helper, relay=relay)
     return PLAN["p"]
 
 
-def send_x_slice(g, core, T, topo, P, info, c0, w, src):
+def common_mask(core, dsts, topo):
+    m = topo.mask(core, dsts[0])
+    for d in dsts:
+        m &= topo.mask(core, d)
+    return engines(m, pow2_le(nbits(m)))
+
+
+def x_transfer(core, T, topo, P, info, c0, w, src):
     col = TC * info["rk"].index(info["r"]) + c0
     peers = [P["cores"][q] for q in info["rk"] if q != info["r"]]
-    m = topo.mask(core, peers[0])
-    for d in peers:
-        m &= topo.mask(core, d)
-    m = engines(m, pow2_le(nbits(m)))
+    m = common_mask(core, peers, topo)
     ids = []
     for d in peers:
         rid, pid = topo.addr(d, core)
         ids.append(DstId(rid=rid, pnc=pid))
-    g.remote_dma_fused([RemoteDMATransfer(dst_ids=ids, dma_engine_mask=m, remote_sem=T.sem.ag, srcs=[src],
-                                          dsts=[T.Wd[:, col:col + w] for d in peers])], local_sem=T.sem.loc)
-    return nbits(m)
+    return RemoteDMATransfer(dst_ids=ids, dma_engine_mask=m, remote_sem=T.sem.ag, srcs=[src],
+                             dsts=[T.Wd[:, col:col + w] for d in peers]), m
+
+
+def mate_transfer(core, T, topo, P, info, e, src):
+    pos = info["rk"].index(info["r"])
+    dsts = info["rdst"][e]
+    m = common_mask(core, dsts, topo)
+    ids = []
+    for d in dsts:
+        rid, pid = topo.addr(d, core)
+        ids.append(DstId(rid=rid, pnc=pid))
+    return RemoteDMATransfer(dst_ids=ids, dma_engine_mask=m, remote_sem=T.sem["rl%d" % pos], srcs=[src],
+                             dsts=[T.Hr[:, XC * pos:XC * (pos + 1)] for d in dsts]), m
 
 
 def send_block_slice(g, core, T, topo, P, info, k, src):
     d = P["cores"][info["partner"]]
-    m = topo.mask(core, d)
-    m = engines(m, pow2_le(nbits(m)))
+    m = common_mask(core, [d], topo)
     rid, pid = topo.addr(d, core)
     g.remote_dma(out_ap=T.Wd[:, 4 * TC + WC * k:4 * TC + WC * (k + 1)], in_ap=src, remote_sem=T.sem["cb%d" % k],
                  local_sem=T.sem.loc, pid=pid, routing_id=rid, dma_engine_mask=m)
@@ -133,55 +180,119 @@ def pair_masks(core, a, b, topo):
     return [engines(full, per, top=0), engines(full, per, top=per)]
 
 
+def hand_mask(rc, info, i, topo):
+    hl = info["hl"]
+    if i < NX - 1:
+        return pair_masks(rc, hl[i - i % 2], hl[i - i % 2 + 1], topo)[i % 2]
+    return common_mask(rc, [hl[i]], topo)
+
+
+PIECES = ([("Sel", 32 * q, 32) for q in range(4)] + [("Mask", 32 * q, 32) for q in range(4)]
+          + [("Jt", 0, 32), ("Jt", 32, 16), ("Jt", 48, 16)])
+
+
+def table_mask(w, rc, P, topo):
+    info = P["ranks"][rc]
+    if w in info["hl"]:
+        i = info["hl"].index(w)
+        later = info["rdst"][i] if i < NM else [P["cores"][q] for q in info["rk"] if q != info["r"]]
+        return common_mask(w, later + [rc], topo)
+    return common_mask(w, [rc], topo)
+
+
+def send_table_piece(g, core, rc, T, topo, P):
+    S, v, A = T.sem, g.vector, AluOpType
+    name, c0, w = PIECES[P["ranks"][rc]["wr"].index(core)]
+    if name == "Sel":
+        g.iota(T.SelI[:, :], [[-1, 128]], 128, 1).then_inc(S.iS, 1)
+        v.wait_ge(S.iS, 1)
+        v.tensor_scalar(T.SelI[:, :], T.SelI[:, :], 15, None, A.bitwise_and).then_inc(S.s1, 1)
+        v.wait_ge(S.s1, 1)
+        v.tensor_scalar(T.Sel[:, :], T.SelI[:, :], 0, None, A.is_equal).then_inc(S.s2, 1)
+        g.wait_ge(S.s2, 1)
+    elif name == "Mask":
+        g.iota(T.MaskI[:, :], [[0, 16], [-16, 8]], 128, 1).then_inc(S.iM, 1)
+        v.wait_ge(S.iM, 1)
+        v.tensor_scalar(T.MaskI[:, :], T.MaskI[:, :], 4, None, A.logical_shift_right).then_inc(S.m1, 1)
+        v.wait_ge(S.m1, 1)
+        v.tensor_scalar(T.Mask[:, :], T.MaskI[:, :], 8, None, A.is_equal).then_inc(S.m2, 1)
+        g.wait_ge(S.m2, 1)
+    else:
+        g.iota(T.Jt[:, 0:64], [[128, 8], [0, 8]], -4096, 1, allow_small_or_imprecise_dtypes=True).then_inc(S.iJ, 1)
+        g.wait_ge(S.iJ, 1)
+    m = table_mask(core, rc, P, topo)
+    rid, pid = topo.addr(rc, core)
+    g.remote_dma(out_ap=T[name][:, c0:c0 + w], in_ap=T[name][:, c0:c0 + w], remote_sem=S.tb, local_sem=S.loc,
+                 pid=pid, routing_id=rid, dma_engine_mask=m)
+    return nbits(m)
+
+
 def rank_program(g, core, T, topo):
     P = plan(T, topo)
     S = T.sem
     if core in P["helper"]:
         rc, i, ck = P["helper"][core]
         info = P["ranks"][rc]
-        car = info["car"]
-        pm = pair_masks(rc, car[i - i % 2], car[i - i % 2 + 1], topo)
-        g.wait_ge(S.hx, nbits(pm[i % 2]))
-        n = send_x_slice(g, core, T, topo, P, info, XC * i, XC, T.Hx[:, :])
+        n = send_table_piece(g, core, rc, T, topo, P)
+        g.wait_ge(S.hx, nbits(hand_mask(rc, info, i, topo)))
+        if i < NM:
+            tr, m = mate_transfer(core, T, topo, P, info, i, T.Hx[:, :])
+        else:
+            tr, m = x_transfer(core, T, topo, P, info, XC * i, XC, T.Hx[:, :])
+        g.remote_dma_fused([tr], local_sem=S.loc)
+        n += nbits(m)
         if ck is not None:
-            g.wait_ge(S.hp, nbits(engines(topo.mask(rc, core), pow2_le(nbits(topo.mask(rc, core))))))
+            g.wait_ge(S.hp, nbits(common_mask(rc, [core], topo)))
             n += send_block_slice(g, core, T, topo, P, info, ck, T.Hp[:, :])
+        g.wait_ge(S.loc, n)
+        return
+    if core in P["relay"]:
+        jobs = sorted(P["relay"][core])
+        n = send_table_piece(g, core, jobs[0][1], T, topo, P)
+        for si, dc, pos, e in jobs:
+            sinfo = P["ranks"][P["cores"][P["ranks"][dc]["rk"][pos]]]
+            g.wait_ge(S["rl%d" % pos], nbits(common_mask(sinfo["hl"][e], sinfo["rdst"][e], topo)))
+            m = common_mask(core, [dc], topo)
+            rid, pid = topo.addr(dc, core)
+            g.remote_dma(out_ap=T.Wd[:, TC * pos + XC * e:TC * pos + XC * (e + 1)], in_ap=T.Hr[:, XC * pos:XC * (pos + 1)],
+                         remote_sem=S.ag, local_sem=S.loc, pid=pid, routing_id=rid, dma_engine_mask=m)
+            n += nbits(m)
         g.wait_ge(S.loc, n)
         return
     if core not in P["ranks"]:
         return
     info = P["ranks"][core]
-    r, rk, pa, car, cab = info["r"], info["rk"], info["partner"], info["car"], info["cab"]
+    r, rk, pa, hl, cab = info["r"], info["rk"], info["partner"], info["hl"], info["cab"]
     own = TC * rk.index(r)
     a = rk[0] * (TC // 16)
     v, pe, sc = g.vector, g.tensor, g.scalar
     A = AluOpType
 
-    for j in range(K):
-        g.sync.dma_start(T.Wd[:, own + WC * j:own + WC * (j + 1)], T.x[:, WC * j:WC * (j + 1)]).then_inc(S["ld%d" % j], 16)
+    for j, (c0, w) in enumerate(LD):
+        g.sync.dma_start(T.Wd[:, own + c0:own + c0 + w], T.x[:, c0:c0 + w]).then_inc(S["ld%d" % j], 16)
     for gi in range(8):
         sc.dma_start(T.G32[16 * gi:16 * gi + 16, :], T.goes[:, a + 32 * gi:a + 32 * gi + 32]).then_inc(S.lg, 16)
 
     g.iota(T.V[:, :], [[1, 512]], -8192, 32, allow_small_or_imprecise_dtypes=True).then_inc(S.iV, 1)
     g.iota(T.Wi8[:, :], [[0, 8]], 0, 1).then_inc(S.iW, 1)
     nloc = 0
-    for j in range(NX // 2):
-        pm = pair_masks(core, car[2 * j], car[2 * j + 1], topo)
+    nag = 0
+    for j, (c0, w) in enumerate(LD):
         trs = []
-        for e in range(2):
-            i = 2 * j + e
-            rid, pid = topo.addr(car[i], core)
-            trs.append(RemoteDMATransfer(dst_ids=[DstId(rid=rid, pnc=pid)], dma_engine_mask=pm[e], remote_sem=S.hx,
-                                         src=T.Wd[:, own + XC * i:own + XC * (i + 1)], dst=T.Hx[:, :]))
-            nloc += nbits(pm[e])
+        for i in range(c0 // XC, (c0 + w) // XC):
+            if i < NX:
+                hm = hand_mask(core, info, i, topo)
+                rid, pid = topo.addr(hl[i], core)
+                trs.append(RemoteDMATransfer(dst_ids=[DstId(rid=rid, pnc=pid)], dma_engine_mask=hm, remote_sem=S.hx,
+                                             src=T.Wd[:, own + XC * i:own + XC * (i + 1)], dst=T.Hx[:, :]))
+                nloc += nbits(hm)
+            else:
+                tr, m = x_transfer(core, T, topo, P, info, XC * i, XC, T.Wd[:, own + XC * i:own + XC * (i + 1)])
+                trs.append(tr)
+                nag = nbits(m)
+                nloc += nag
         g.wait_ge(S["ld%d" % j], 16)
         g.remote_dma_fused(trs, local_sem=S.loc)
-    g.wait_ge(S["ld%d" % (K - 1)], 16)
-    nag = send_x_slice(g, core, T, topo, P, info, XC * NX, TC - XC * NX, T.Wd[:, own + XC * NX:own + TC])
-    nloc += nag
-    g.iota(T.Jt[:, 0:64], [[128, 8], [0, 8]], -4096, 1, allow_small_or_imprecise_dtypes=True).then_inc(S.iJ, 1)
-    g.iota(T.MaskI[:, :], [[0, 16], [-16, 8]], 128, 1).then_inc(S.iM, 1)
-    g.iota(T.SelI[:, :], [[-1, 128]], 128, 1).then_inc(S.iS, 1)
 
     v.memset(T.Wi[:, TC * pa:TC * pa + TC], 0.0).then_inc(S.mB, 1)
     v.memset(T.Wi[:, TC * r:TC * r + TC], 0.0).then_inc(S.mA, 1)
@@ -205,31 +316,25 @@ def rank_program(g, core, T, topo):
             pe.matmul(T.PS1[:, 64 * li + 8 * b:64 * li + 8 * b + 8], T.Wi[:, base + 128 * b:base + 128 * b + 128],
                       T.Wsel[:, :], True, True).then_inc(S.pe1, 1)
 
-    v.wait_ge(S.iM, 1)
-    v.tensor_scalar(T.MaskI[:, :], T.MaskI[:, :], 4, None, A.logical_shift_right).then_inc(S.m1, 1)
-    v.wait_ge(S.iS, 1)
-    v.tensor_scalar(T.SelI[:, :], T.SelI[:, :], 15, None, A.bitwise_and).then_inc(S.s1, 1)
-    v.wait_ge(S.m1, 1)
-    v.tensor_scalar(T.Mask[:, :], T.MaskI[:, :], 8, None, A.is_equal).then_inc(S.m2, 1)
-    v.wait_ge(S.s1, 1)
-    v.tensor_scalar(T.Sel[:, :], T.SelI[:, :], 0, None, A.is_equal).then_inc(S.s2, 1)
+    ntb = sum(nbits(table_mask(m, core, P, topo)) for m in info["wr"])
     v.wait_ge(S.pe1, 16)
-    v.wait_ge(S.iJ, 1)
+    v.wait_ge(S.tb, ntb)
     v.wait_ge(S.j2, 1)
     v.tensor_tensor(T.R1[:, :], T.PS1[:, 0:128], T.Jt[:, :], A.min).then_inc(S.r1, 1)
     v.wait_ge(S.r1, 1)
-    v.wait_ge(S.m2, 1)
     v.tensor_tensor(T.R2[:, :], T.R1[:, :], T.Mask[:, :], A.mult).then_inc(S.r2, 1)
     pe.wait_ge(S.r2, 1)
-    pe.wait_ge(S.s2, 1)
+    pe.wait_ge(S.tb, ntb)
     pe.matmul(T.PS2[:, 0:128], T.Sel[:, :], T.R2[:, :], True, True).then_inc(S.pe2, 1)
     v.wait_ge(S.pe2, 1)
     v.tensor_scalar(T.offAB[:, :], T.PS2[:, 0:128], 8192, None, A.add).then_inc(S.ob, 1)
 
-    nall = 3 * (NX + 1) * nag
+    nrel = sum(nbits(common_mask(m, [core], topo)) * len(P["relay"][m]) for side in info["rel"].values() for m in side
+               if m in P["relay"])
+    nall = 3 * (NX + 1 - NM) * nag + nrel
     for q in (v, sc):
         q.wait_ge(S.ob, 1)
-        for j in range(K):
+        for j in range(len(LD)):
             q.wait_ge(S["ld%d" % j], 16)
         q.wait_ge(S.ag, nall)
     oc = WC // 16
@@ -240,12 +345,12 @@ def rank_program(g, core, T, topo):
             v.tensor_copy(out, src).then_inc(S["gb%d" % k], 1)
         else:
             sc.activation(out, src, ActivationFunctionType.Copy).then_inc(S["gb%d" % k], 1)
+    ncb = 0
     for k in range(K):
         g.wait_ge(S["gb%d" % k], 1)
         if k < K - 1:
-            h = cab[k]
-            m = engines(topo.mask(core, h), pow2_le(nbits(topo.mask(core, h))))
-            rid, pid = topo.addr(h, core)
+            m = common_mask(core, [cab[k]], topo)
+            rid, pid = topo.addr(cab[k], core)
             g.remote_dma(out_ap=T.Hp[:, :], in_ap=T.Pb[:, WC * k:WC * (k + 1)], remote_sem=S.hp, local_sem=S.loc,
                          pid=pid, routing_id=rid, dma_engine_mask=m)
             nloc += nbits(m)

from concourse.bass import DstId, RemoteDMATransfer
from concourse.mybir import AluOpType, ActivationFunctionType

N = 8
TC = 1024
NSIM = 512
K = 4
WC = TC // K
NX = 7
NM = 2
XC = 128
LD = [(0, 2 * XC), (2 * XC, 2 * XC), (4 * XC, 2 * XC), (6 * XC, XC), (7 * XC, XC)]

SCRATCH = {
    "Wd": ("sbuf", [128, 5 * TC], "float32"),
    "Pb": ("sbuf", [128, TC], "float32"),
    "Y": ("sbuf", [128, TC], "float32"),
    "Hx": ("sbuf", [128, XC], "float32"),
    "Hr": ("sbuf", [128, 4 * XC], "float32"),
    "Hp": ("sbuf", [128, WC], "float32"),
    "G32": ("sbuf", [128, 32], "int32"),
    "off16": ("sbuf", [128, 32], "uint16"),
    "V": ("sbuf", [128, 512], "float32"),
    "Wi": ("sbuf", [128, N * TC], "float32"),
    "Wi8": ("sbuf", [128, 8], "int32"),
    "Wsel": ("sbuf", [128, 8], "float32"),
    "SelI": ("sbuf", [128, 128], "int32"),
    "Sel": ("sbuf", [128, 128], "float32"),
    "MaskI": ("sbuf", [128, 128], "int32"),
    "Mask": ("sbuf", [128, 128], "float32"),
    "Jt": ("sbuf", [128, 128], "float32"),
    "R1": ("sbuf", [128, 128], "float32"),
    "R2": ("sbuf", [128, 128], "float32"),
    "offAB": ("sbuf", [128, 128], "uint16"),
    "PS1": ("psum", [128, 512], "float32"),
    "PS2": ("psum", [128, 512], "float32"),
}
SEMAPHORES = (["lg", "iV", "iW", "iS", "iM", "iJ", "mA", "mB", "w1", "w2", "o1", "sc", "pe1", "s1", "s2",
               "m1", "m2", "j2", "r1", "r2", "pe2", "ob", "ag", "hx", "hp", "loc", "rl0", "rl1", "rl2", "rl3", "tb"]
              + ["ld%d" % k for k in range(len(LD))]
              + ["%s%d" % (n, k) for n in ("gb", "cb", "ga", "st") for k in range(K)])

PLAN = {}


def engines(mask, count, top=0):
    bits = [b for b in range(16) if (mask >> b) & 1]
    bits = bits[len(bits) - top - count:len(bits) - top]
    return sum(1 << b for b in bits)


def pow2_le(n):
    p = 1
    while p * 2 <= n:
        p *= 2
    return p


def nbits(mask):
    return sum((mask >> b) & 1 for b in range(16))


def plan(T, topo):
    if "p" in PLAN:
        return PLAN["p"]
    cores = [int(c) for c in T.cores]
    ranks, helper = {}, {}
    for r, c in enumerate(cores):
        rk = [q for q in range(N) if topo.rack(topo.host(cores[q])) == topo.rack(topo.host(c))]
        pa = [q for q in range(N) if q not in rk and topo.chip(cores[q]) == topo.chip(c) and topo.may_write(c, cores[q])]
        assert len(pa) == 1 and rk == list(range(rk[0], rk[0] + len(rk))) and len(rk) == 4
        assert all(topo.same_plane(c, cores[q]) for q in rk if q != r)
        hostc = [m for m in range(NSIM) if topo.host(m) == topo.host(c)]
        chipc = [m for m in hostc if topo.chip(m) == topo.chip(c)]
        kd = {}
        for k in chipc:
            kd[k] = (topo.die(k), any(topo.may_write(k, m) for m in hostc if topo.mates(k, m)))
        far = [m for m in chipc if topo.die(m) != topo.die(c)]
        near = [m for m in chipc if topo.die(m) == topo.die(c) and m != c]
        near = [m for m in near if kd[m] != kd[c]] + [m for m in near if kd[m] == kd[c]]
        fk = []
        for m in far:
            if kd[m] not in fk:
                fk.append(kd[m])
        far2, left = [], list(far)
        while left:
            for q in fk:
                mine = [m for m in left if kd[m] == q]
                if mine:
                    far2.append(mine[0])
                    left.remove(mine[0])
        snd = [[m for m in side if kd[m][1]][0] for side in (far2, near)]
        fr = [m for m in far2 if m not in snd]
        nr = [m for m in near if m not in snd]
        car = []
        while fr or nr:
            for side in (fr, nr):
                if side:
                    car.append(side.pop(0))
        hl = snd + car
        assert len(snd) == NM and len(hl) == NX
        cab, seen = [], [kd[c]]
        for m in hl:
            if kd[m] not in seen:
                seen.append(kd[m])
                cab.append(m)
        assert len(cab) == K - 1
        rel = {}
        for m in hostc:
            if topo.mates(m, c) and topo.may_write(m, c):
                rel.setdefault(topo.die(m), []).append(m)
        wr = hl + sorted(m for side in rel.values() for m in side)
        assert len(wr) == len(PIECES)
        ranks[c] = dict(r=r, rk=rk, partner=pa[0], hl=hl, cab=cab, rel=rel, rdst={}, wr=wr)
        for i, h in enumerate(hl):
            helper[h] = (c, i, cab.index(h) if h in cab else None)
    relay = {}
    for c, info in ranks.items():
        r, rk = info["r"], info["rk"]
        for e in range(NM):
            sd = topo.die(info["hl"][e])
            info["rdst"][e] = []
            for d in rk:
                if d == r:
                    continue
                dc = cores[d]
                si = [q for q in rk if q != d].index(r)
                lst = ranks[dc]["rel"][sd]
                m = lst[si % len(lst)]
                assert topo.may_write(info["hl"][e], m)
                info["rdst"][e].append(m)
                relay.setdefault(m, []).append((si, dc, rk.index(r), e))
    PLAN["p"] = dict(cores=cores, ranks=ranks, helper=helper, relay=relay)
    return PLAN["p"]


def common_mask(core, dsts, topo):
    m = topo.mask(core, dsts[0])
    for d in dsts:
        m &= topo.mask(core, d)
    return engines(m, pow2_le(nbits(m)))


def x_transfer(core, T, topo, P, info, c0, w, src):
    col = TC * info["rk"].index(info["r"]) + c0
    peers = [P["cores"][q] for q in info["rk"] if q != info["r"]]
    m = common_mask(core, peers, topo)
    ids = []
    for d in peers:
        rid, pid = topo.addr(d, core)
        ids.append(DstId(rid=rid, pnc=pid))
    return RemoteDMATransfer(dst_ids=ids, dma_engine_mask=m, remote_sem=T.sem.ag, srcs=[src],
                             dsts=[T.Wd[:, col:col + w] for d in peers]), m


def mate_transfer(core, T, topo, P, info, e, src):
    pos = info["rk"].index(info["r"])
    dsts = info["rdst"][e]
    m = common_mask(core, dsts, topo)
    ids = []
    for d in dsts:
        rid, pid = topo.addr(d, core)
        ids.append(DstId(rid=rid, pnc=pid))
    return RemoteDMATransfer(dst_ids=ids, dma_engine_mask=m, remote_sem=T.sem["rl%d" % pos], srcs=[src],
                             dsts=[T.Hr[:, XC * pos:XC * (pos + 1)] for d in dsts]), m


def send_block_slice(g, core, T, topo, P, info, k, src):
    d = P["cores"][info["partner"]]
    m = common_mask(core, [d], topo)
    rid, pid = topo.addr(d, core)
    g.remote_dma(out_ap=T.Wd[:, 4 * TC + WC * k:4 * TC + WC * (k + 1)], in_ap=src, remote_sem=T.sem["cb%d" % k],
                 local_sem=T.sem.loc, pid=pid, routing_id=rid, dma_engine_mask=m)
    return nbits(m)


def pair_masks(core, a, b, topo):
    full = topo.mask(core, a) & topo.mask(core, b)
    per = pow2_le(nbits(full) // 2)
    return [engines(full, per, top=0), engines(full, per, top=per)]


def hand_mask(rc, info, i, topo):
    hl = info["hl"]
    if i < NX - 1:
        return pair_masks(rc, hl[i - i % 2], hl[i - i % 2 + 1], topo)[i % 2]
    return common_mask(rc, [hl[i]], topo)


PIECES = ([("Sel", 32 * q, 32) for q in range(4)] + [("Mask", 32 * q, 32) for q in range(4)]
          + [("Jt", 0, 32), ("Jt", 32, 16), ("Jt", 48, 16)])


def table_mask(w, rc, P, topo):
    info = P["ranks"][rc]
    if w in info["hl"]:
        i = info["hl"].index(w)
        later = info["rdst"][i] if i < NM else [P["cores"][q] for q in info["rk"] if q != info["r"]]
        return common_mask(w, later + [rc], topo)
    return common_mask(w, [rc], topo)


def send_table_piece(g, core, rc, T, topo, P):
    S, v, A = T.sem, g.vector, AluOpType
    name, c0, w = PIECES[P["ranks"][rc]["wr"].index(core)]
    if name == "Sel":
        g.iota(T.SelI[:, :], [[-1, 128]], 128, 1).then_inc(S.iS, 1)
        v.wait_ge(S.iS, 1)
        v.tensor_scalar(T.SelI[:, :], T.SelI[:, :], 15, None, A.bitwise_and).then_inc(S.s1, 1)
        v.wait_ge(S.s1, 1)
        v.tensor_scalar(T.Sel[:, :], T.SelI[:, :], 0, None, A.is_equal).then_inc(S.s2, 1)
        g.wait_ge(S.s2, 1)
    elif name == "Mask":
        g.iota(T.MaskI[:, :], [[0, 16], [-16, 8]], 128, 1).then_inc(S.iM, 1)
        v.wait_ge(S.iM, 1)
        v.tensor_scalar(T.MaskI[:, :], T.MaskI[:, :], 4, None, A.logical_shift_right).then_inc(S.m1, 1)
        v.wait_ge(S.m1, 1)
        v.tensor_scalar(T.Mask[:, :], T.MaskI[:, :], 8, None, A.is_equal).then_inc(S.m2, 1)
        g.wait_ge(S.m2, 1)
    else:
        g.iota(T.Jt[:, 0:64], [[128, 8], [0, 8]], -4096, 1, allow_small_or_imprecise_dtypes=True).then_inc(S.iJ, 1)
        g.wait_ge(S.iJ, 1)
    m = table_mask(core, rc, P, topo)
    rid, pid = topo.addr(rc, core)
    g.remote_dma(out_ap=T[name][:, c0:c0 + w], in_ap=T[name][:, c0:c0 + w], remote_sem=S.tb, local_sem=S.loc,
                 pid=pid, routing_id=rid, dma_engine_mask=m)
    return nbits(m)


def rank_program(g, core, T, topo):
    P = plan(T, topo)
    S = T.sem
    if core in P["helper"]:
        rc, i, ck = P["helper"][core]
        info = P["ranks"][rc]
        n = send_table_piece(g, core, rc, T, topo, P)
        g.wait_ge(S.hx, nbits(hand_mask(rc, info, i, topo)))
        if i < NM:
            tr, m = mate_transfer(core, T, topo, P, info, i, T.Hx[:, :])
        else:
            tr, m = x_transfer(core, T, topo, P, info, XC * i, XC, T.Hx[:, :])
        g.remote_dma_fused([tr], local_sem=S.loc)
        n += nbits(m)
        if ck is not None:
            g.wait_ge(S.hp, nbits(common_mask(rc, [core], topo)))
            n += send_block_slice(g, core, T, topo, P, info, ck, T.Hp[:, :])
        g.wait_ge(S.loc, n)
        return
    if core in P["relay"]:
        jobs = sorted(P["relay"][core])
        n = send_table_piece(g, core, jobs[0][1], T, topo, P)
        for si, dc, pos, e in jobs:
            sinfo = P["ranks"][P["cores"][P["ranks"][dc]["rk"][pos]]]
            g.wait_ge(S["rl%d" % pos], nbits(common_mask(sinfo["hl"][e], sinfo["rdst"][e], topo)))
            m = common_mask(core, [dc], topo)
            rid, pid = topo.addr(dc, core)
            g.remote_dma(out_ap=T.Wd[:, TC * pos + XC * e:TC * pos + XC * (e + 1)], in_ap=T.Hr[:, XC * pos:XC * (pos + 1)],
                         remote_sem=S.ag, local_sem=S.loc, pid=pid, routing_id=rid, dma_engine_mask=m)
            n += nbits(m)
        g.wait_ge(S.loc, n)
        return
    if core not in P["ranks"]:
        return
    info = P["ranks"][core]
    r, rk, pa, hl, cab = info["r"], info["rk"], info["partner"], info["hl"], info["cab"]
    own = TC * rk.index(r)
    a = rk[0] * (TC // 16)
    v, pe, sc = g.vector, g.tensor, g.scalar
    A = AluOpType

    for j, (c0, w) in enumerate(LD):
        g.sync.dma_start(T.Wd[:, own + c0:own + c0 + w], T.x[:, c0:c0 + w]).then_inc(S["ld%d" % j], 16)
    for gi in range(8):
        sc.dma_start(T.G32[16 * gi:16 * gi + 16, :], T.goes[:, a + 32 * gi:a + 32 * gi + 32]).then_inc(S.lg, 16)

    g.iota(T.V[:, :], [[1, 512]], -8192, 32, allow_small_or_imprecise_dtypes=True).then_inc(S.iV, 1)
    g.iota(T.Wi8[:, :], [[0, 8]], 0, 1).then_inc(S.iW, 1)
    nloc = 0
    nag = 0
    for j, (c0, w) in enumerate(LD):
        trs = []
        for i in range(c0 // XC, (c0 + w) // XC):
            if i < NX:
                hm = hand_mask(core, info, i, topo)
                rid, pid = topo.addr(hl[i], core)
                trs.append(RemoteDMATransfer(dst_ids=[DstId(rid=rid, pnc=pid)], dma_engine_mask=hm, remote_sem=S.hx,
                                             src=T.Wd[:, own + XC * i:own + XC * (i + 1)], dst=T.Hx[:, :]))
                nloc += nbits(hm)
            else:
                tr, m = x_transfer(core, T, topo, P, info, XC * i, XC, T.Wd[:, own + XC * i:own + XC * (i + 1)])
                trs.append(tr)
                nag = nbits(m)
                nloc += nag
        g.wait_ge(S["ld%d" % j], 16)
        g.remote_dma_fused(trs, local_sem=S.loc)

    v.memset(T.Wi[:, TC * pa:TC * pa + TC], 0.0).then_inc(S.mB, 1)
    v.memset(T.Wi[:, TC * r:TC * r + TC], 0.0).then_inc(S.mA, 1)
    v.memset(T.Jt[:, 64:128], -4097.0).then_inc(S.j2, 1)
    v.wait_ge(S.iW, 1)
    v.tensor_scalar(T.Wi8[:, :], T.Wi8[:, :], 15, None, A.bitwise_and).then_inc(S.w1, 1)
    v.wait_ge(S.w1, 1)
    v.tensor_scalar(T.Wsel[:, :], T.Wi8[:, :], 0, None, A.is_equal).then_inc(S.w2, 1)
    v.wait_ge(S.lg, 128)
    v.tensor_copy(T.off16[:, :], T.G32[:, :]).then_inc(S.o1, 1)
    v.wait_ge(S.o1, 1)
    v.wait_ge(S.iV, 1)
    v.wait_ge(S.mA, 1)
    v.wait_ge(S.mB, 1)
    v.tensor_copy(T.Wi[:, 0:N * TC].indirect(T.off16[:, 0:32]), T.V[:, :]).then_inc(S.sc, 1)

    pe.wait_ge(S.sc, 1)
    pe.wait_ge(S.w2, 1)
    for li, base in enumerate((TC * r, TC * pa)):
        for b in range(8):
            pe.matmul(T.PS1[:, 64 * li + 8 * b:64 * li + 8 * b + 8], T.Wi[:, base + 128 * b:base + 128 * b + 128],
                      T.Wsel[:, :], True, True).then_inc(S.pe1, 1)

    ntb = sum(nbits(table_mask(m, core, P, topo)) for m in info["wr"])
    v.wait_ge(S.pe1, 16)
    v.wait_ge(S.tb, ntb)
    v.wait_ge(S.j2, 1)
    v.tensor_tensor(T.R1[:, :], T.PS1[:, 0:128], T.Jt[:, :], A.min).then_inc(S.r1, 1)
    v.wait_ge(S.r1, 1)
    v.tensor_tensor(T.R2[:, :], T.R1[:, :], T.Mask[:, :], A.mult).then_inc(S.r2, 1)
    pe.wait_ge(S.r2, 1)
    pe.wait_ge(S.tb, ntb)
    pe.matmul(T.PS2[:, 0:128], T.Sel[:, :], T.R2[:, :], True, True).then_inc(S.pe2, 1)
    v.wait_ge(S.pe2, 1)
    v.tensor_scalar(T.offAB[:, :], T.PS2[:, 0:128], 8192, None, A.add).then_inc(S.ob, 1)

    nrel = sum(nbits(common_mask(m, [core], topo)) * len(P["relay"][m]) for side in info["rel"].values() for m in side
               if m in P["relay"])
    nall = 3 * (NX + 1 - NM) * nag + nrel
    for q in (v, sc):
        q.wait_ge(S.ob, 1)
        for j in range(len(LD)):
            q.wait_ge(S["ld%d" % j], 16)
        q.wait_ge(S.ag, nall)
    oc = WC // 16
    for k in range(K):
        out = T.Pb[:, WC * k:WC * (k + 1)]
        src = T.Wd[:, 0:4 * TC].indirect(T.offAB[:, 64 + oc * k:64 + oc * (k + 1)])
        if k % 2 == 0:
            v.tensor_copy(out, src).then_inc(S["gb%d" % k], 1)
        else:
            sc.activation(out, src, ActivationFunctionType.Copy).then_inc(S["gb%d" % k], 1)
    ncb = 0
    for k in range(K):
        g.wait_ge(S["gb%d" % k], 1)
        if k < K - 1:
            m = common_mask(core, [cab[k]], topo)
            rid, pid = topo.addr(cab[k], core)
            g.remote_dma(out_ap=T.Hp[:, :], in_ap=T.Pb[:, WC * k:WC * (k + 1)], remote_sem=S.hp, local_sem=S.loc,
                         pid=pid, routing_id=rid, dma_engine_mask=m)
            nloc += nbits(m)
        else:
            ncb = send_block_slice(g, core, T, topo, P, info, k, T.Pb[:, WC * k:WC * (k + 1)])
            nloc += ncb

    waited = {0: 0, 1: 0}
    for k in range(K):
        e = k % 2
        q = v if e == 0 else sc
        for kk in range(waited[e], k + 1):
            q.wait_ge(S["cb%d" % kk], ncb)
        waited[e] = k + 1
        out = T.Y[:, WC * k:WC * (k + 1)]
        src = T.Wd[:, 0:4 * TC + WC * (k + 1)].indirect(T.offAB[:, oc * k:oc * (k + 1)])
        if e == 0:
            v.tensor_copy(out, src).then_inc(S["ga%d" % k], 1)
        else:
            sc.activation(out, src, ActivationFunctionType.Copy).then_inc(S["ga%d" % k], 1)
        d = g.sync if e == 0 else sc
        d.wait_ge(S["ga%d" % k], 1)
        d.dma_start(T.y[:, WC * k:WC * (k + 1)], T.Y[:, WC * k:WC * (k + 1)]).then_inc(S["st%d" % k], 16)
    g.wait_ge(S.loc, nloc)
    for k in range(K):
        g.wait_ge(S["st%d" % k], 16)
